import numpy as np
import ml_dtypes


def mxq(x, axis, fmt="e4m3"):
    dtype, down = {"e4m3": (ml_dtypes.float8_e4m3fn, 7), "e5m2": (ml_dtypes.float8_e5m2, 14)}[fmt]
    v = np.moveaxis(np.asarray(x, np.float32).astype(ml_dtypes.bfloat16).astype(np.float64), axis, -1)
    blocks = v.reshape(v.shape[:-1] + (-1, 32))
    amax = np.abs(blocks).max(-1, keepdims=True)
    byte = np.maximum(np.where(amax > 0, np.frexp(amax)[1] - 1 + 127, 0) - down, 1)
    scale = np.exp2(byte - 127.0)
    codes = (blocks / scale).astype(np.float32).astype(dtype).astype(np.float64)
    return np.moveaxis((codes * scale).reshape(v.shape), -1, axis)


WIDE = False


def mx_kscale(k):
    if not WIDE:
        return np.ones(k)
    levels = np.array([10, -10, 5, -5, 0])
    if k % 512:
        return np.exp2(np.random.permutation(np.resize(levels, k // 32))).repeat(32)
    a = np.empty((k // 512, 16))
    for p in range(k // 512):
        a[p, :8] = np.random.permutation(np.resize(levels, 8))
        for g in range(8):
            far = levels[np.abs(levels - a[p, g]) >= 10]
            a[p, g + 8] = far[np.random.randint(len(far))]
    return np.exp2(a.ravel()).repeat(32)


def f64(x):
    return np.asarray(x).astype(np.float64)


def striped(idx):
    return np.tile(np.asarray(idx).reshape(-1, 16).T, (8, 1)).astype(np.uint16)


def unstriped(offs):
    return offs[:16].T.reshape(-1).astype(np.int64)


def striped8(idx):
    return np.asarray(idx).reshape(8, -1, 16).transpose(0, 2, 1).reshape(128, -1).astype(np.uint16)


def unstriped8(offs):
    return offs.reshape(8, 16, -1).transpose(0, 2, 1).reshape(8, -1).astype(np.int64)


def pick8(x, idx, run):
    r = np.arange(len(x))
    return x[r[:, None], idx[r % (8 * run) // run]]


E2M1 = np.array([0.0, 0.5, 1.0, 1.5, 2.0, 3.0, 4.0, 6.0, -0.0, -0.5, -1.0, -1.5, -2.0, -3.0, -4.0, -6.0])


def pack_weight(w, fmt):
    k, n = w.shape
    w = f64(np.asarray(w, np.float32).astype(ml_dtypes.bfloat16)).reshape(k // 32, 32, n)
    amax = np.abs(w).max(1)
    if fmt == "e4m3":
        byte = np.frexp(amax)[1] - 1 + 127 - 7
    else:
        mant, ex = np.frexp(amax / 6.0)
        byte = np.where(mant > 0.5, ex, ex - 1) + 127
    byte = np.clip(np.where(amax > 0, byte, 1), 1, 254)
    scaled = (w * np.exp2(127.0 - byte)[:, None, :]).reshape(k, n).astype(np.float32)
    by_word = np.ascontiguousarray(scaled.reshape(k // 512, 128, 4, n).transpose(0, 1, 3, 2))
    if fmt == "e4m3":
        words = by_word.astype(ml_dtypes.float8_e4m3fn).view(np.uint8)
    else:
        c = by_word.astype(ml_dtypes.float4_e2m1fn).view(np.uint8) & 0xF
        words = (c[..., 0::2] | (c[..., 1::2] << 4)).reshape(k // 512, 128, 2 * n)
    return np.ascontiguousarray(words), np.ascontiguousarray(byte.astype(np.uint8).reshape(k // 512, 16, n))


def unpack_weight(words, scales, fmt):
    g, _, n = scales.shape
    words = np.ascontiguousarray(words).reshape(g, 128, n, -1)
    if fmt == "e4m3":
        vals = words.view(ml_dtypes.float8_e4m3fn).astype(np.float64)
    else:
        nib = np.empty((g, 128, n, 4), np.uint8)
        nib[..., 0::2] = words & 0xF
        nib[..., 1::2] = words >> 4
        vals = E2M1[nib]
    vals = vals * np.repeat(np.exp2(scales.astype(np.float64) - 127.0), 8, axis=1)[..., None]
    return vals.transpose(0, 1, 3, 2).reshape(g * 512, n)


K, J, R, T, U, Z, M, O, C, N, S, V = 512, 256, 512, 512, 512, 512, 1024, 128, 512, 256, 512, 1024


def setup_inputs():
    n = np.random.standard_normal
    idx = np.random.permutation(T)[:J]
    idx2 = np.stack([np.random.permutation(U)[:J] for _ in range(8)])
    idx3 = np.random.permutation(M)[:J]
    idx4 = np.stack([np.random.permutation(C)[:J] for _ in range(8)])
    idx5 = np.stack([np.random.permutation(C)[:O] for _ in range(8)])
    idx6 = np.stack([np.random.permutation(J)[:O] for _ in range(8)])
    idx7 = np.random.permutation(V)[:O]
    fk = mx_kscale(K)
    fr = mx_kscale(R)
    fz = mx_kscale(Z)
    fs = mx_kscale(S)
    wp = pack_weight(n((K, R)) * 1 / np.sqrt(K) / fk[:, None] * fr, "e4m3")
    xop = pack_weight(n((Z, M)) / fz[:, None], "e4m3")
    w2p = pack_weight(n((Z, R)) * 1 / np.sqrt(Z) * fz[:, None] * fr, "e2m1")
    wbp = pack_weight(n((R, N)) * 1 / np.sqrt(R) / fr[:, None], "e2m1")
    xrp = pack_weight(n((S, V)) / fs[:, None], "e4m3")
    wsp = pack_weight(n((S, N)) * 1 / np.sqrt(S) * fs[:, None], "e4m3")
    return {
        "ta": (np.random.randint(-7, 8, (K, T)).astype(np.float64)).astype(np.float32),
        "tb": (np.random.randint(-7, 8, (K, U)).astype(np.float64)).astype(np.float32),
        "ga": ((np.random.randint(10, 25, (K, 1)) / 64.0) * fk[:, None]).astype(np.float32),
        "gb": ((np.random.randint(4, 13, (K, 1)) / 64.0) * fk[:, None]).astype(np.float32),
        "w_words": wp[0],
        "w_scales": wp[1],
        "xo_words": xop[0],
        "xo_scales": xop[1],
        "w2_words": w2p[0],
        "w2_scales": w2p[1],
        "sa": (np.random.uniform(0.5, 1.6, (R, 1))).astype(np.float32),
        "sb": (np.random.uniform(0.5, 1.6, (R, 1))).astype(np.float32),
        "wb_words": wbp[0],
        "wb_scales": wbp[1],
        "xr_words": xrp[0],
        "xr_scales": xrp[1],
        "ws_words": wsp[0],
        "ws_scales": wsp[1],
        "offs": striped(idx),
        "offs2": striped8(idx2),
        "offs3": striped(idx3),
        "offs4": striped8(idx4),
        "offs5": striped8(idx5),
        "offs6": striped8(idx6),
        "offs7": striped(idx7),
    }


def reference(ta, tb, ga, gb, w_words, w_scales, xo_words, xo_scales, w2_words, w2_scales, sa, sb, wb_words, wb_scales, xr_words, xr_scales, ws_words, ws_scales, offs, offs2, offs3, offs4, offs5, offs6, offs7):
    idx = unstriped(offs)
    idx2 = unstriped8(offs2)
    idx3 = unstriped(offs3)
    idx4 = unstriped8(offs4)
    idx5 = unstriped8(offs5)
    idx6 = unstriped8(offs6)
    idx7 = unstriped(offs7)
    wu = unpack_weight(w_words, w_scales, "e4m3")
    xou = unpack_weight(xo_words, xo_scales, "e4m3")
    w2u = unpack_weight(w2_words, w2_scales, "e2m1")
    wbu = unpack_weight(wb_words, wb_scales, "e2m1")
    xru = unpack_weight(xr_words, xr_scales, "e4m3")
    wsu = unpack_weight(ws_words, ws_scales, "e4m3")
    xc = f64(ta)[:, idx] * f64(ga) + pick8(f64(tb), idx2, 64) * f64(gb)
    xcq = mxq(xc, 0, "e4m3")
    a = wu.T @ xcq
    xoidx3g = xou[:, idx3]
    b = w2u.T @ xoidx3g
    pw = np.zeros((R, C))
    pw[np.arange(R)[:, None], idx4[np.arange(R) % 512 // 64]] = a
    hid = np.maximum(pick8(pw, idx5, 64) * f64(sa), pick8(b, idx6, 64) * f64(sb))
    hidq = mxq(hid, 0, "e4m3")
    xridx7g = xru[:, idx7]
    y = wbu.T @ hidq + wsu.T @ xridx7g
    return y

@@ -1,0 +1,240 @@
+from contextlib import ExitStack
+
+import concourse.mybir as mybir
+
+F32 = mybir.dt.float32
+BF16 = mybir.dt.bfloat16
+I32 = mybir.dt.int32
+U32 = mybir.dt.uint32
+U16 = mybir.dt.uint16
+U8 = mybir.dt.uint8
+FP8X4 = mybir.dt.float8_e4m3fn_x4
+FP4X4 = mybir.dt.float4_e2m1fn_x4
+COPY = mybir.ActivationFunctionType.Copy
+ADD = mybir.AluOpType.add
+MAX = mybir.AluOpType.max
+
+P = 128
+PACK = 4
+QUADS = 4
+J, R, T, M, O, C, N, V = 256, 512, 512, 1024, 128, 512, 256, 1024
+HALF = J // 2
+FLOPS = 335544320
+
+
+def tile_picked_basedetail_plain_two_boardmeet_reminder_plain_kernel(
+    tc, ta, tb, ga, gb, w_words, w_scales, xo_words, xo_scales, w2_words, w2_scales, sa, sb,
+    wb_words, wb_scales, xr_words, xr_scales, ws_words, ws_scales,
+    offs, offs2, offs3, offs4, offs5, offs6, offs7, out,
+):
+    nc = tc.nc
+    with ExitStack() as ctx:
+        sbuf = ctx.enter_context(tc.tile_pool(name="sbuf", bufs=1))
+        psum = ctx.enter_context(tc.psum_pool(name="psum", bufs=1))
+
+        def tile(shape, dtype, name):
+            return sbuf.tile(shape, dtype, name=name, align_bytes=64)
+
+        def load_list(src, name):
+            lst = tile(list(src.shape), U16, name)
+            nc.sync.dma_start(lst[:], src)
+            return lst
+
+        def load_column(queue, src, name):
+            col = tile([P, PACK], F32, name)
+            queue.dma_start(col[:], src.rearrange("(p t) o -> p (t o)", t=PACK))
+            return col
+
+        def load_words(src, name):
+            words = tile([P, src.shape[2]], I32, name)
+            nc.sync.dma_start(words[:], src[0].rearrange("p n t -> p (n t)").bitcast(I32))
+            return words
+
+        def by_quadrant(scales):
+            return scales[0].bitcast(I32).rearrange("(q i) n -> i q n", i=4)
+
+        ta_rows = ta.rearrange("(p t) c -> t p c", t=PACK)
+        tb_rows = tb.rearrange("(p t) c -> t p c", t=PACK)
+        ta_sb = [tile([P, T], F32, "ta%d" % t) for t in range(PACK)]
+        tb_sb = [tile([P, T], F32, "tb%d" % t) for t in range(PACK)]
+
+        w_stage = tile([32, QUADS, R // 4], I32, "w_stage")
+        nc.vector.memset(w_stage[:], 0)
+        xo_plane = tile([P, M], U8, "xo_plane")
+        nc.vector.memset(xo_plane[:].bitcast(I32), 0)
+        xr_plane = tile([P, V], U8, "xr_plane")
+        nc.vector.memset(xr_plane[:].bitcast(I32), 0)
+        out_planes = tile([P, 2 * N], U8, "out_planes")
+        nc.vector.memset(out_planes[:].bitcast(I32), 0)
+        board = [tile([P, C], F32, "board%d" % t) for t in range(PACK)]
+        for t in range(PACK):
+            nc.vector.memset(board[t][:], 0.0)
+
+        ga_sb = load_column(nc.scalar, ga, "ga_sb")
+        gb_sb = load_column(nc.scalar, gb, "gb_sb")
+        nc.sync.dma_start(ta_sb[0][:], ta_rows[0])
+        l1 = load_list(offs, "l1")
+        nc.sync.dma_start(tb_sb[0][:], tb_rows[0])
+        l2 = load_list(offs2, "l2")
+        nc.sync.dma_start(ta_sb[1][:], ta_rows[1])
+        nc.sync.dma_start(tb_sb[1][:], tb_rows[1])
+        l3 = load_list(offs3, "l3")
+        for t in (2, 3):
+            nc.sync.dma_start(ta_sb[t][:], ta_rows[t])
+            nc.sync.dma_start(tb_sb[t][:], tb_rows[t])
+        w_sb = load_words(w_words, "w_sb")
+        l4 = load_list(offs4, "l4")
+        xo_sb = load_words(xo_words, "xo_sb")
+        w2_sb = tile([P, 2 * R], U8, "w2_sb")
+        nc.sync.dma_start(w2_sb[:].bitcast(I32), w2_words[0].bitcast(I32))
+        l6 = load_list(offs6, "l6")
+        sb_sb = load_column(nc.sync, sb, "sb_sb")
+        l5 = load_list(offs5, "l5")
+        sa_sb = load_column(nc.sync, sa, "sa_sb")
+        l7 = load_list(offs7, "l7")
+        for q in range(QUADS):
+            nc.sync.dma_start(xr_plane[32 * q : 32 * q + 4, :].bitcast(I32), xr_scales[0, 4 * q : 4 * q + 4, :].bitcast(I32))
+        xr_sb = load_words(xr_words, "xr_sb")
+        ws_sb = load_words(ws_words, "ws_sb")
+        wb_sb = tile([P, 2 * N], U8, "wb_sb")
+        nc.sync.dma_start(wb_sb[:].bitcast(I32), wb_words[0].bitcast(I32))
+        for q in range(QUADS):
+            rows = out_planes[32 * q : 32 * q + 4, :].bitcast(I32)
+            nc.sync.dma_start(rows[:, 0 : N // 4], wb_scales[0, 4 * q : 4 * q + 4, :].bitcast(I32))
+            nc.sync.dma_start(rows[:, N // 4 : N // 2], ws_scales[0, 4 * q : 4 * q + 4, :].bitcast(I32))
+
+        xo_stage = tile([4, QUADS, M // 4], I32, "xo_stage")
+        nc.gpsimd.dma_start(xo_stage[:], by_quadrant(xo_scales))
+        nc.gpsimd.dma_start(w_stage[0:4], by_quadrant(w2_scales))
+        nc.gpsimd.dma_start(w_stage[4:8], by_quadrant(w_scales))
+
+        for q in range(QUADS):
+            nc.vector.tensor_copy(xo_plane[32 * q : 32 * q + 4, :].bitcast(I32), xo_stage[:, q, :])
+        xo_sc = tile([P, J], U8, "xo_sc")
+        nc.vector.tensor_copy(xo_sc[:], xo_plane[:].indirect(l3[:]))
+        w_planes = tile([P, R], U8, "w_planes")
+        for q in range(QUADS):
+            nc.vector.tensor_copy(w_planes[32 * q : 32 * q + 32, :].bitcast(I32), w_stage[:, q, :])
+        w_planes_dealt = tile([P, R], U8, "w_planes_dealt")
+        nc.vector.tensor_copy(
+            w_planes_dealt[:].rearrange("p (t m) -> p t m", t=PACK),
+            w_planes[:].rearrange("p (m t) -> p t m", t=PACK),
+        )
+
+        base = [tile([P, J], F32, "base%d" % t) for t in range(PACK)]
+        detail = [tile([P, J], F32, "detail%d" % t) for t in range(PACK)]
+        xc = [tile([P, PACK, HALF], F32, "xc%d" % h) for h in range(2)]
+        last = PACK - 1
+        for t in range(PACK):
+            nc.scalar.activation(out=base[t][:], in_=ta_sb[t][:].indirect(l1[:]), func=COPY, scale=ga_sb[:, t : t + 1])
+            if t < last:
+                nc.scalar.activation(out=detail[t][:], in_=tb_sb[t][:].indirect(l2[:]), func=COPY, scale=gb_sb[:, t : t + 1])
+                for h in range(2):
+                    cols = slice(h * HALF, (h + 1) * HALF)
+                    nc.vector.tensor_tensor(xc[h][:, t, :], base[t][:, cols], detail[t][:, cols], ADD)
+        for h in range(2):
+            cols = slice(h * HALF, (h + 1) * HALF)
+            nc.scalar.activation(
+                out=detail[last][:, cols], in_=tb_sb[last][:].indirect(l2[:, 8 * h : 8 * h + 8]), func=COPY,
+                scale=gb_sb[:, last : last + 1],
+            )
+
+        w_dealt = tile([P, R], U32, "w_dealt")
+        nc.scalar.copy(
+            w_dealt[:].rearrange("p (t m) -> p t m", t=PACK),
+            w_sb[:].bitcast(U32).rearrange("p (m t) -> p t m", t=PACK),
+        )
+
+        xc_bf = [tile([P, HALF * PACK], BF16, "xc_bf%d" % h) for h in range(2)]
+        xc_codes = [tile([P, HALF], U32, "xc_codes%d" % h) for h in range(2)]
+        xc_sc = [tile([P, HALF], U8, "xc_sc%d" % h) for h in range(2)]
+        for h in range(2):
+            cols = slice(h * HALF, (h + 1) * HALF)
+            nc.vector.tensor_tensor(xc[h][:, last, :], base[last][:, cols], detail[last][:, cols], ADD)
+            nc.vector.tensor_copy(
+                xc_bf[h][:].rearrange("p (c i t) -> p c t i", i=4, t=PACK),
+                xc[h][:].rearrange("p t (c i) -> p c t i", i=4),
+            )
+            nc.vector.quantize_mx(out=xc_codes[h][:].bitcast(FP8X4), scales=xc_sc[h][:], in_=xc_bf[h][:])
+
+        xo_codes = tile([P, J], U32, "xo_codes")
+        nc.vector.tensor_copy(xo_codes[:], xo_sb[:].bitcast(U32).indirect(l3[:]))
+
+        a_sb = {}
+        for h, planes in ((0, (0,)), (0, (1, 2, 3)), (1, (0, 1, 2, 3))):
+            name = "a%d_%d" % (h, planes[0])
+            acc = psum.tile([P, len(planes), HALF], F32, name="ps_" + name)
+            for s, t in enumerate(planes):
+                cols = slice(t * P, (t + 1) * P)
+                nc.tensor.matmul_mx(
+                    out=acc[:, s, :], lhsT=w_dealt[:, cols].bitcast(FP8X4), lhsT_scale=w_planes_dealt[4:P, cols],
+                    rhs=xc_codes[h][:].bitcast(FP8X4), rhs_scale=xc_sc[h][:], start=True, stop=True,
+                )
+            res = tile([P, len(planes), HALF], F32, name)
+            nc.scalar.copy(res[:], acc[:])
+            for s, t in enumerate(planes):
+                a_sb[(h, t)] = res[:, s, :]
+
+        w2_dealt = tile([P, 2 * R], U8, "w2_dealt")
+        nc.scalar.copy(
+            w2_dealt[:].bitcast(U16).rearrange("p (t m) -> p t m", t=PACK),
+            w2_sb[:].bitcast(U16).rearrange("p (m t) -> p t m", t=PACK),
+        )
+        second = tile([P, PACK, O], F32, "second")
+        for pair in range(2):
+            acc = psum.tile([P, 2, J], F32, name="ps_b%d" % pair)
+            for s in range(2):
+                t = 2 * pair + s
+                nc.tensor.matmul_mx(
+                    out=acc[:, s, :], lhsT=w2_dealt[:, 2 * P * t : 2 * P * (t + 1)].bitcast(FP4X4),
+                    lhsT_scale=w_planes_dealt[:, t * P : (t + 1) * P],
+                    rhs=xo_codes[:].bitcast(FP8X4), rhs_scale=xo_sc[:], start=True, stop=True,
+                )
+            for s in range(2):
+                t = 2 * pair + s
+                b_sb = tile([P, J], F32, "b%d" % t)
+                nc.scalar.copy(b_sb[:], acc[:, s, :])
+                nc.scalar.activation(out=second[:, t, :], in_=b_sb[:].indirect(l6[:]), func=COPY, scale=sb_sb[:, t : t + 1])
+
+        first = tile([P, PACK, O], F32, "first")
+        for h in range(2):
+            for t in range(PACK):
+                nc.vector.tensor_copy(board[t][:].indirect(l4[:, 8 * h : 8 * h + 8]), a_sb[(h, t)])
+                if h == 1:
+                    nc.scalar.activation(out=first[:, t, :], in_=board[t][:].indirect(l5[:]), func=COPY, scale=sa_sb[:, t : t + 1])
+
+        xr_sc = tile([P, O], U8, "xr_sc")
+        nc.vector.tensor_copy(xr_sc[:], xr_plane[:].indirect(l7[:]))
+        xr_codes = tile([P, O], U32, "xr_codes")
+        nc.vector.tensor_copy(xr_codes[:], xr_sb[:].bitcast(U32).indirect(l7[:]))
+        accs = [psum.tile([P, O], F32, name="ps_y%d" % u) for u in range(2)]
+        for u in range(2):
+            nc.tensor.matmul_mx(
+                out=accs[u][:], lhsT=ws_sb[:, u * P : (u + 1) * P].bitcast(FP8X4),
+                lhsT_scale=out_planes[:, N + u * P : N + (u + 1) * P],
+                rhs=xr_codes[:].bitcast(FP8X4), rhs_scale=xr_sc[:], start=True, stop=False,
+            )
+
+        hid_bf = tile([P, O * PACK], BF16, "hid_bf")
+        nc.vector.tensor_tensor(
+            hid_bf[:].rearrange("p (c i t) -> p c t i", i=4, t=PACK),
+            first[:].rearrange("p t (c i) -> p c t i", i=4),
+            second[:].rearrange("p t (c i) -> p c t i", i=4),
+            MAX,
+        )
+        hid_codes = tile([P, O], U32, "hid_codes")
+        hid_sc = tile([P, O], U8, "hid_sc")
+        nc.vector.quantize_mx(out=hid_codes[:].bitcast(FP8X4), scales=hid_sc[:], in_=hid_bf[:])
+
+        for u in range(2):
+            nc.tensor.matmul_mx(
+                out=accs[u][:], lhsT=wb_sb[:, 2 * P * u : 2 * P * (u + 1)].bitcast(FP4X4),
+                lhsT_scale=out_planes[:, u * P : (u + 1) * P],
+                rhs=hid_codes[:].bitcast(FP8X4), rhs_scale=hid_sc[:], start=False, stop=True,
+            )
+        y0 = tile([P, O], F32, "y0")
+        nc.vector.tensor_copy(y0[:], accs[0][:])
+        nc.sync.dma_start(out[0:P, :], y0[:])
+        y1 = tile([P, O], F32, "y1")
+        nc.scalar.copy(y1[:], accs[1][:])
+        nc.scalar.dma_start(out[P : 2 * P, :], y1[:])

@@ -32,8 +32,8 @@ def tile_picked_basedetail_plain_two_boardmeet_reminder_plain_kernel(
         sbuf = ctx.enter_context(tc.tile_pool(name="sbuf", bufs=1))
         psum = ctx.enter_context(tc.psum_pool(name="psum", bufs=1))
 
-        def tile(shape, dtype, name):
-            return sbuf.tile(shape, dtype, name=name, align_bytes=64)
+        def tile(shape, dtype, name, tag=None):
+            return sbuf.tile(shape, dtype, name=name, tag=tag or name, align_bytes=64)
 
         def load_list(src, name):
             lst = tile(list(src.shape), U16, name)
@@ -50,18 +50,20 @@ def tile_picked_basedetail_plain_two_boardmeet_reminder_plain_kernel(
             nc.sync.dma_start(words[:], src[0].rearrange("p n t -> p (n t)").bitcast(I32))
             return words
 
-        def by_quadrant(scales):
-            return scales[0].bitcast(I32).rearrange("(q i) n -> i q n", i=4)
+        def load_scale_rows(queue, plane, scales, q):
+            queue.dma_start(plane[32 * q : 32 * q + 4, :].bitcast(I32), scales[0, 4 * q : 4 * q + 4, :].bitcast(I32))
 
         ta_rows = ta.rearrange("(p t) c -> t p c", t=PACK)
         tb_rows = tb.rearrange("(p t) c -> t p c", t=PACK)
         ta_sb = [tile([P, T], F32, "ta%d" % t) for t in range(PACK)]
         tb_sb = [tile([P, T], F32, "tb%d" % t) for t in range(PACK)]
 
-        w_stage = tile([32, QUADS, R // 4], I32, "w_stage")
-        nc.vector.memset(w_stage[:], 0)
+        w2_plane = tile([P, R], U8, "w2_plane")
+        nc.vector.memset(w2_plane[:].bitcast(I32), 0)
         xo_plane = tile([P, M], U8, "xo_plane")
         nc.vector.memset(xo_plane[:].bitcast(I32), 0)
+        w_plane = tile([P, R], U8, "w_plane")
+        nc.vector.memset(w_plane[:].bitcast(I32), 0)
         xr_plane = tile([P, V], U8, "xr_plane")
         nc.vector.memset(xr_plane[:].bitcast(I32), 0)
         out_planes = tile([P, 2 * N], U8, "out_planes")
@@ -78,22 +80,32 @@ def tile_picked_basedetail_plain_two_boardmeet_reminder_plain_kernel(
         l2 = load_list(offs2, "l2")
         nc.sync.dma_start(ta_sb[1][:], ta_rows[1])
         nc.sync.dma_start(tb_sb[1][:], tb_rows[1])
-        l3 = load_list(offs3, "l3")
-        for t in (2, 3):
-            nc.sync.dma_start(ta_sb[t][:], ta_rows[t])
-            nc.sync.dma_start(tb_sb[t][:], tb_rows[t])
+        nc.sync.dma_start(ta_sb[2][:], ta_rows[2])
+        load_scale_rows(nc.sync, w_plane, w_scales, 0)
+        load_scale_rows(nc.sync, w_plane, w_scales, 1)
+        nc.sync.dma_start(tb_sb[2][:], tb_rows[2])
+        load_scale_rows(nc.sync, w_plane, w_scales, 2)
+        load_scale_rows(nc.sync, w_plane, w_scales, 3)
+        nc.sync.dma_start(ta_sb[3][:], ta_rows[3])
+        nc.sync.dma_start(tb_sb[3][:], tb_rows[3])
+        for q in range(QUADS):
+            load_scale_rows(nc.gpsimd, w2_plane, w2_scales, q)
         w_sb = load_words(w_words, "w_sb")
-        l4 = load_list(offs4, "l4")
+        l3 = load_list(offs3, "l3")
+        load_scale_rows(nc.sync, xo_plane, xo_scales, 0)
         xo_sb = load_words(xo_words, "xo_sb")
+        for q in range(1, QUADS):
+            load_scale_rows(nc.sync, xo_plane, xo_scales, q)
         w2_sb = tile([P, 2 * R], U8, "w2_sb")
         nc.sync.dma_start(w2_sb[:].bitcast(I32), w2_words[0].bitcast(I32))
+        l4 = load_list(offs4, "l4")
         l6 = load_list(offs6, "l6")
         sb_sb = load_column(nc.sync, sb, "sb_sb")
         l5 = load_list(offs5, "l5")
         sa_sb = load_column(nc.sync, sa, "sa_sb")
         l7 = load_list(offs7, "l7")
         for q in range(QUADS):
-            nc.sync.dma_start(xr_plane[32 * q : 32 * q + 4, :].bitcast(I32), xr_scales[0, 4 * q : 4 * q + 4, :].bitcast(I32))
+            load_scale_rows(nc.sync, xr_plane, xr_scales, q)
         xr_sb = load_words(xr_words, "xr_sb")
         ws_sb = load_words(ws_words, "ws_sb")
         wb_sb = tile([P, 2 * N], U8, "wb_sb")
@@ -103,40 +115,27 @@ def tile_picked_basedetail_plain_two_boardmeet_reminder_plain_kernel(
             nc.sync.dma_start(rows[:, 0 : N // 4], wb_scales[0, 4 * q : 4 * q + 4, :].bitcast(I32))
             nc.sync.dma_start(rows[:, N // 4 : N // 2], ws_scales[0, 4 * q : 4 * q + 4, :].bitcast(I32))
 
-        xo_stage = tile([4, QUADS, M // 4], I32, "xo_stage")
-        nc.gpsimd.dma_start(xo_stage[:], by_quadrant(xo_scales))
-        nc.gpsimd.dma_start(w_stage[0:4], by_quadrant(w2_scales))
-        nc.gpsimd.dma_start(w_stage[4:8], by_quadrant(w_scales))
 
-        for q in range(QUADS):
-            nc.vector.tensor_copy(xo_plane[32 * q : 32 * q + 4, :].bitcast(I32), xo_stage[:, q, :])
-        xo_sc = tile([P, J], U8, "xo_sc")
-        nc.vector.tensor_copy(xo_sc[:], xo_plane[:].indirect(l3[:]))
-        w_planes = tile([P, R], U8, "w_planes")
-        for q in range(QUADS):
-            nc.vector.tensor_copy(w_planes[32 * q : 32 * q + 32, :].bitcast(I32), w_stage[:, q, :])
-        w_planes_dealt = tile([P, R], U8, "w_planes_dealt")
-        nc.vector.tensor_copy(
-            w_planes_dealt[:].rearrange("p (t m) -> p t m", t=PACK),
-            w_planes[:].rearrange("p (m t) -> p t m", t=PACK),
-        )
+        def deal_plane(plane, name, tag=None):
+            dealt = tile([P, R], U8, name, tag)
+            nc.vector.tensor_copy(
+                dealt[:].rearrange("p (t m) -> p t m", t=PACK), plane[:].rearrange("p (m t) -> p t m", t=PACK)
+            )
+            return dealt
 
-        base = [tile([P, J], F32, "base%d" % t) for t in range(PACK)]
-        detail = [tile([P, J], F32, "detail%d" % t) for t in range(PACK)]
-        xc = [tile([P, PACK, HALF], F32, "xc%d" % h) for h in range(2)]
+        w_plane_dealt = deal_plane(w_plane, "w_plane_dealt")
+
+        base = tile([P, PACK, J], F32, "base")
+        detail = tile([P, PACK, J], F32, "detail")
         last = PACK - 1
         for t in range(PACK):
-            nc.scalar.activation(out=base[t][:], in_=ta_sb[t][:].indirect(l1[:]), func=COPY, scale=ga_sb[:, t : t + 1])
+            nc.scalar.activation(out=base[:, t, :], in_=ta_sb[t][:].indirect(l1[:]), func=COPY, scale=ga_sb[:, t : t + 1])
             if t < last:
-                nc.scalar.activation(out=detail[t][:], in_=tb_sb[t][:].indirect(l2[:]), func=COPY, scale=gb_sb[:, t : t + 1])
-                for h in range(2):
-                    cols = slice(h * HALF, (h + 1) * HALF)
-                    nc.vector.tensor_tensor(xc[h][:, t, :], base[t][:, cols], detail[t][:, cols], ADD)
+                nc.scalar.activation(out=detail[:, t, :], in_=tb_sb[t][:].indirect(l2[:]), func=COPY, scale=gb_sb[:, t : t + 1])
         for h in range(2):
-            cols = slice(h * HALF, (h + 1) * HALF)
             nc.scalar.activation(
-                out=detail[last][:, cols], in_=tb_sb[last][:].indirect(l2[:, 8 * h : 8 * h + 8]), func=COPY,
-                scale=gb_sb[:, last : last + 1],
+                out=detail[:, last, h * HALF : (h + 1) * HALF], in_=tb_sb[last][:].indirect(l2[:, 8 * h : 8 * h + 8]),
+                func=COPY, scale=gb_sb[:, last : last + 1],
             )
 
         w_dealt = tile([P, R], U32, "w_dealt")
@@ -145,37 +144,46 @@ def tile_picked_basedetail_plain_two_boardmeet_reminder_plain_kernel(
             w_sb[:].bitcast(U32).rearrange("p (m t) -> p t m", t=PACK),
         )
 
-        xc_bf = [tile([P, HALF * PACK], BF16, "xc_bf%d" % h) for h in range(2)]
-        xc_codes = [tile([P, HALF], U32, "xc_codes%d" % h) for h in range(2)]
-        xc_sc = [tile([P, HALF], U8, "xc_sc%d" % h) for h in range(2)]
+        xc_bf = tile([P, J * PACK], BF16, "xc_bf")
+        nc.vector.tensor_tensor(
+            xc_bf[:].rearrange("p (c i t) -> p c t i", i=4, t=PACK)[:, :, 0:last, :],
+            base[:, 0:last, :].rearrange("p t (c i) -> p c t i", i=4),
+            detail[:, 0:last, :].rearrange("p t (c i) -> p c t i", i=4),
+            ADD,
+        )
+        xc_codes = tile([P, J], U32, "xc_codes")
+        xc_sc = tile([P, J], U8, "xc_sc")
         for h in range(2):
             cols = slice(h * HALF, (h + 1) * HALF)
-            nc.vector.tensor_tensor(xc[h][:, last, :], base[last][:, cols], detail[last][:, cols], ADD)
-            nc.vector.tensor_copy(
-                xc_bf[h][:].rearrange("p (c i t) -> p c t i", i=4, t=PACK),
-                xc[h][:].rearrange("p t (c i) -> p c t i", i=4),
+            nc.vector.tensor_tensor(
+                xc_bf[:].rearrange("p (j t) -> p j t", t=PACK)[:, cols, last], base[:, last, cols], detail[:, last, cols], ADD
             )
-            nc.vector.quantize_mx(out=xc_codes[h][:].bitcast(FP8X4), scales=xc_sc[h][:], in_=xc_bf[h][:])
+        for h in range(2):
+            cols = slice(h * HALF, (h + 1) * HALF)
+            nc.vector.quantize_mx(
+                out=xc_codes[:, cols].bitcast(FP8X4), scales=xc_sc[:, cols],
+                in_=xc_bf[:, h * HALF * PACK : (h + 1) * HALF * PACK],
+            )
 
+        w2_plane_dealt = deal_plane(w2_plane, "w2_plane_dealt", "xc_bf")
         xo_codes = tile([P, J], U32, "xo_codes")
         nc.vector.tensor_copy(xo_codes[:], xo_sb[:].bitcast(U32).indirect(l3[:]))
+        xo_sc = tile([P, J], U8, "xo_sc")
+        nc.vector.tensor_copy(xo_sc[:], xo_plane[:].indirect(l3[:]))
 
-        a_sb = {}
-        for h, planes in ((0, (0,)), (0, (1, 2, 3)), (1, (0, 1, 2, 3))):
-            name = "a%d_%d" % (h, planes[0])
-            acc = psum.tile([P, len(planes), HALF], F32, name="ps_" + name)
-            for s, t in enumerate(planes):
-                cols = slice(t * P, (t + 1) * P)
-                nc.tensor.matmul_mx(
-                    out=acc[:, s, :], lhsT=w_dealt[:, cols].bitcast(FP8X4), lhsT_scale=w_planes_dealt[4:P, cols],
-                    rhs=xc_codes[h][:].bitcast(FP8X4), rhs_scale=xc_sc[h][:], start=True, stop=True,
-                )
-            res = tile([P, len(planes), HALF], F32, name)
+        a_sb = []
+        for t in range(PACK):
+            cols = slice(t * P, (t + 1) * P)
+            acc = psum.tile([P, J], F32, name="ps_a%d" % t)
+            nc.tensor.matmul_mx(
+                out=acc[:], lhsT=w_dealt[:, cols].bitcast(FP8X4), lhsT_scale=w_plane_dealt[:, cols],
+                rhs=xc_codes[:].bitcast(FP8X4), rhs_scale=xc_sc[:], start=True, stop=True,
+            )
+            res = tile([P, J], F32, "a%d" % t)
             nc.scalar.copy(res[:], acc[:])
-            for s, t in enumerate(planes):
-                a_sb[(h, t)] = res[:, s, :]
+            a_sb.append(res)
 
-        w2_dealt = tile([P, 2 * R], U8, "w2_dealt")
+        w2_dealt = tile([P, 2 * R], U8, "w2_dealt", "xc_codes")
         nc.scalar.copy(
             w2_dealt[:].bitcast(U16).rearrange("p (t m) -> p t m", t=PACK),
             w2_sb[:].bitcast(U16).rearrange("p (m t) -> p t m", t=PACK),
@@ -187,7 +195,7 @@ def tile_picked_basedetail_plain_two_boardmeet_reminder_plain_kernel(
                 t = 2 * pair + s
                 nc.tensor.matmul_mx(
                     out=acc[:, s, :], lhsT=w2_dealt[:, 2 * P * t : 2 * P * (t + 1)].bitcast(FP4X4),
-                    lhsT_scale=w_planes_dealt[:, t * P : (t + 1) * P],
+                    lhsT_scale=w2_plane_dealt[:, t * P : (t + 1) * P],
                     rhs=xo_codes[:].bitcast(FP8X4), rhs_scale=xo_sc[:], start=True, stop=True,
                 )
             for s in range(2):
@@ -196,16 +204,14 @@ def tile_picked_basedetail_plain_two_boardmeet_reminder_plain_kernel(
                 nc.scalar.copy(b_sb[:], acc[:, s, :])
                 nc.scalar.activation(out=second[:, t, :], in_=b_sb[:].indirect(l6[:]), func=COPY, scale=sb_sb[:, t : t + 1])
 
-        first = tile([P, PACK, O], F32, "first")
-        for h in range(2):
-            for t in range(PACK):
-                nc.vector.tensor_copy(board[t][:].indirect(l4[:, 8 * h : 8 * h + 8]), a_sb[(h, t)])
-                if h == 1:
-                    nc.scalar.activation(out=first[:, t, :], in_=board[t][:].indirect(l5[:]), func=COPY, scale=sa_sb[:, t : t + 1])
+        first = tile([P, PACK, O], F32, "first", "b3")
+        for t in range(PACK):
+            nc.vector.tensor_copy(board[t][:].indirect(l4[:]), a_sb[t][:])
+            nc.scalar.activation(out=first[:, t, :], in_=board[t][:].indirect(l5[:]), func=COPY, scale=sa_sb[:, t : t + 1])
 
-        xr_sc = tile([P, O], U8, "xr_sc")
+        xr_sc = tile([P, O], U8, "xr_sc", "a2")
         nc.vector.tensor_copy(xr_sc[:], xr_plane[:].indirect(l7[:]))
-        xr_codes = tile([P, O], U32, "xr_codes")
+        xr_codes = tile([P, O], U32, "xr_codes", "a3")
         nc.vector.tensor_copy(xr_codes[:], xr_sb[:].bitcast(U32).indirect(l7[:]))
         accs = [psum.tile([P, O], F32, name="ps_y%d" % u) for u in range(2)]
         for u in range(2):

@@ -58,6 +58,10 @@ def tile_picked_basedetail_plain_two_boardmeet_reminder_plain_kernel(
         ta_sb = [tile([P, T], F32, "ta%d" % t) for t in range(PACK)]
         tb_sb = [tile([P, T], F32, "tb%d" % t) for t in range(PACK)]
 
+        warm_in = tile([P, 1], F32, "warm_in")
+        nc.vector.memset(warm_in[:], 0.0)
+        warm_out = tile([P, 1], F32, "warm_out")
+        nc.scalar.activation(out=warm_out[:], in_=warm_in[:], func=COPY)
         w2_plane = tile([P, R], U8, "w2_plane")
         nc.vector.memset(w2_plane[:].bitcast(I32), 0)
         xo_plane = tile([P, M], U8, "xo_plane")

from contextlib import ExitStack

import concourse.mybir as mybir

F32 = mybir.dt.float32
BF16 = mybir.dt.bfloat16
I32 = mybir.dt.int32
U32 = mybir.dt.uint32
U16 = mybir.dt.uint16
U8 = mybir.dt.uint8
FP8X4 = mybir.dt.float8_e4m3fn_x4
FP4X4 = mybir.dt.float4_e2m1fn_x4
COPY = mybir.ActivationFunctionType.Copy
ADD = mybir.AluOpType.add
MAX = mybir.AluOpType.max

P = 128
PACK = 4
QUADS = 4
J, R, T, M, O, C, N, V = 256, 512, 512, 1024, 128, 512, 256, 1024
HALF = J // 2
FLOPS = 335544320


def tile_picked_basedetail_plain_two_boardmeet_reminder_plain_kernel(
    tc, ta, tb, ga, gb, w_words, w_scales, xo_words, xo_scales, w2_words, w2_scales, sa, sb,
    wb_words, wb_scales, xr_words, xr_scales, ws_words, ws_scales,
    offs, offs2, offs3, offs4, offs5, offs6, offs7, out,
):
    nc = tc.nc
    with ExitStack() as ctx:
        sbuf = ctx.enter_context(tc.tile_pool(name="sbuf", bufs=1))
        psum = ctx.enter_context(tc.psum_pool(name="psum", bufs=1))

        def tile(shape, dtype, name, tag=None):
            return sbuf.tile(shape, dtype, name=name, tag=tag or name, align_bytes=64)

        def load_list(src, name):
            lst = tile(list(src.shape), U16, name)
            nc.sync.dma_start(lst[:], src)
            return lst

        def load_column(queue, src, name):
            col = tile([P, PACK], F32, name)
            queue.dma_start(col[:], src.rearrange("(p t) o -> p (t o)", t=PACK))
            return col

        def load_words(src, name):
            words = tile([P, src.shape[2]], I32, name)
            nc.sync.dma_start(words[:], src[0].rearrange("p n t -> p (n t)").bitcast(I32))
            return words

        def load_scale_rows(queue, plane, scales, q):
            queue.dma_start(plane[32 * q : 32 * q + 4, :].bitcast(I32), scales[0, 4 * q : 4 * q + 4, :].bitcast(I32))

        ta_rows = ta.rearrange("(p t) c -> t p c", t=PACK)
        tb_rows = tb.rearrange("(p t) c -> t p c", t=PACK)
        ta_sb = [tile([P, T], F32, "ta%d" % t) for t in range(PACK)]
        tb_sb = [tile([P, T], F32, "tb%d" % t) for t in range(PACK)]

        warm_in = tile([P, 1], F32, "warm_in")
        nc.vector.memset(warm_in[:], 0.0)
        warm_out = tile([P, 1], F32, "warm_out")
        nc.scalar.activation(out=warm_out[:], in_=warm_in[:], func=COPY)
        w2_plane = tile([P, R], U8, "w2_plane")
        nc.vector.memset(w2_plane[:].bitcast(I32), 0)
        xo_plane = tile([P, M], U8, "xo_plane")
        nc.vector.memset(xo_plane[:].bitcast(I32), 0)
        w_plane = tile([P, R], U8, "w_plane")
        nc.vector.memset(w_plane[:].bitcast(I32), 0)
        xr_plane = tile([P, V], U8, "xr_plane")
        nc.vector.memset(xr_plane[:].bitcast(I32), 0)
        out_planes = tile([P, 2 * N], U8, "out_planes")
        nc.vector.memset(out_planes[:].bitcast(I32), 0)
        board = [tile([P, C], F32, "board%d" % t) for t in range(PACK)]
        for t in range(PACK):
            nc.vector.memset(board[t][:], 0.0)

        ga_sb = load_column(nc.scalar, ga, "ga_sb")
        gb_sb = load_column(nc.scalar, gb, "gb_sb")
        nc.sync.dma_start(ta_sb[0][:], ta_rows[0])
        l1 = load_list(offs, "l1")
        nc.sync.dma_start(tb_sb[0][:], tb_rows[0])
        l2 = load_list(offs2, "l2")
        nc.sync.dma_start(ta_sb[1][:], ta_rows[1])
        nc.sync.dma_start(tb_sb[1][:], tb_rows[1])
        nc.sync.dma_start(ta_sb[2][:], ta_rows[2])
        load_scale_rows(nc.sync, w_plane, w_scales, 0)
        load_scale_rows(nc.sync, w_plane, w_scales, 1)
        nc.sync.dma_start(tb_sb[2][:], tb_rows[2])
        load_scale_rows(nc.sync, w_plane, w_scales, 2)
        load_scale_rows(nc.sync, w_plane, w_scales, 3)
        nc.sync.dma_start(ta_sb[3][:], ta_rows[3])
        nc.sync.dma_start(tb_sb[3][:], tb_rows[3])
        for q in range(QUADS):
            load_scale_rows(nc.gpsimd, w2_plane, w2_scales, q)
        w_sb = load_words(w_words, "w_sb")
        l3 = load_list(offs3, "l3")
        load_scale_rows(nc.sync, xo_plane, xo_scales, 0)
        xo_sb = load_words(xo_words, "xo_sb")
        for q in range(1, QUADS):
            load_scale_rows(nc.sync, xo_plane, xo_scales, q)
        w2_sb = tile([P, 2 * R], U8, "w2_sb")
        nc.sync.dma_start(w2_sb[:].bitcast(I32), w2_words[0].bitcast(I32))
        l4 = load_list(offs4, "l4")
        l6 = load_list(offs6, "l6")
        sb_sb = load_column(nc.sync, sb, "sb_sb")
        l5 = load_list(offs5, "l5")
        sa_sb = load_column(nc.sync, sa, "sa_sb")
        l7 = load_list(offs7, "l7")
        for q in range(QUADS):
            load_scale_rows(nc.sync, xr_plane, xr_scales, q)
        xr_sb = load_words(xr_words, "xr_sb")
        ws_sb = load_words(ws_words, "ws_sb")
        wb_sb = tile([P, 2 * N], U8, "wb_sb")
        nc.sync.dma_start(wb_sb[:].bitcast(I32), wb_words[0].bitcast(I32))
        for q in range(QUADS):
            rows = out_planes[32 * q : 32 * q + 4, :].bitcast(I32)
            nc.sync.dma_start(rows[:, 0 : N // 4], wb_scales[0, 4 * q : 4 * q + 4, :].bitcast(I32))
            nc.sync.dma_start(rows[:, N // 4 : N // 2], ws_scales[0, 4 * q : 4 * q + 4, :].bitcast(I32))


        def deal_plane(plane, name, tag=None):
            dealt = tile([P, R], U8, name, tag)
            nc.vector.tensor_copy(
                dealt[:].rearrange("p (t m) -> p t m", t=PACK), plane[:].rearrange("p (m t) -> p t m", t=PACK)
            )
            return dealt

        w_plane_dealt = deal_plane(w_plane, "w_plane_dealt")

        base = tile([P, PACK, J], F32, "base")
        detail = tile([P, PACK, J], F32, "detail")
        last = PACK - 1
        for t in range(PACK):
            nc.scalar.activation(out=base[:, t, :], in_=ta_sb[t][:].indirect(l1[:]), func=COPY, scale=ga_sb[:, t : t + 1])
            if t < last:
                nc.scalar.activation(out=detail[:, t, :], in_=tb_sb[t][:].indirect(l2[:]), func=COPY, scale=gb_sb[:, t : t + 1])
        for h in range(2):
            nc.scalar.activation(
                out=detail[:, last, h * HALF : (h + 1) * HALF], in_=tb_sb[last][:].indirect(l2[:, 8 * h : 8 * h + 8]),
                func=COPY, scale=gb_sb[:, last : last + 1],
            )

        w_dealt = tile([P, R], U32, "w_dealt")
        nc.scalar.copy(
            w_dealt[:].rearrange("p (t m) -> p t m", t=PACK),
            w_sb[:].bitcast(U32).rearrange("p (m t) -> p t m", t=PACK),
        )

        xc_bf = tile([P, J * PACK], BF16, "xc_bf")
        nc.vector.tensor_tensor(
            xc_bf[:].rearrange("p (c i t) -> p c t i", i=4, t=PACK)[:, :, 0:last, :],
            base[:, 0:last, :].rearrange("p t (c i) -> p c t i", i=4),
            detail[:, 0:last, :].rearrange("p t (c i) -> p c t i", i=4),
            ADD,
        )
        xc_codes = tile([P, J], U32, "xc_codes")
        xc_sc = tile([P, J], U8, "xc_sc")
        for h in range(2):
            cols = slice(h * HALF, (h + 1) * HALF)
            nc.vector.tensor_tensor(
                xc_bf[:].rearrange("p (j t) -> p j t", t=PACK)[:, cols, last], base[:, last, cols], detail[:, last, cols], ADD
            )
        for h in range(2):
            cols = slice(h * HALF, (h + 1) * HALF)
            nc.vector.quantize_mx(
                out=xc_codes[:, cols].bitcast(FP8X4), scales=xc_sc[:, cols],
                in_=xc_bf[:, h * HALF * PACK : (h + 1) * HALF * PACK],
            )

        w2_plane_dealt = deal_plane(w2_plane, "w2_plane_dealt", "xc_bf")
        xo_codes = tile([P, J], U32, "xo_codes")
        nc.vector.tensor_copy(xo_codes[:], xo_sb[:].bitcast(U32).indirect(l3[:]))
        xo_sc = tile([P, J], U8, "xo_sc")
        nc.vector.tensor_copy(xo_sc[:], xo_plane[:].indirect(l3[:]))

        a_sb = []
        for t in range(PACK):
            cols = slice(t * P, (t + 1) * P)
            acc = psum.tile([P, J], F32, name="ps_a%d" % t)
            nc.tensor.matmul_mx(
                out=acc[:], lhsT=w_dealt[:, cols].bitcast(FP8X4), lhsT_scale=w_plane_dealt[:, cols],
                rhs=xc_codes[:].bitcast(FP8X4), rhs_scale=xc_sc[:], start=True, stop=True,
            )
            res = tile([P, J], F32, "a%d" % t)
            nc.scalar.copy(res[:], acc[:])
            a_sb.append(res)

        w2_dealt = tile([P, 2 * R], U8, "w2_dealt", "xc_codes")
        nc.scalar.copy(
            w2_dealt[:].bitcast(U16).rearrange("p (t m) -> p t m", t=PACK),
            w2_sb[:].bitcast(U16).rearrange("p (m t) -> p t m", t=PACK),
        )
        second = tile([P, PACK, O], F32, "second")
        for pair in range(2):
            acc = psum.tile([P, 2, J], F32, name="ps_b%d" % pair)
            for s in range(2):
                t = 2 * pair + s
                nc.tensor.matmul_mx(
                    out=acc[:, s, :], lhsT=w2_dealt[:, 2 * P * t : 2 * P * (t + 1)].bitcast(FP4X4),
                    lhsT_scale=w2_plane_dealt[:, t * P : (t + 1) * P],
                    rhs=xo_codes[:].bitcast(FP8X4), rhs_scale=xo_sc[:], start=True, stop=True,
                )
            for s in range(2):
                t = 2 * pair + s
                b_sb = tile([P, J], F32, "b%d" % t)
                nc.scalar.copy(b_sb[:], acc[:, s, :])
                nc.scalar.activation(out=second[:, t, :], in_=b_sb[:].indirect(l6[:]), func=COPY, scale=sb_sb[:, t : t + 1])

        first = tile([P, PACK, O], F32, "first", "b3")
        for t in range(PACK):
            nc.vector.tensor_copy(board[t][:].indirect(l4[:]), a_sb[t][:])
            nc.scalar.activation(out=first[:, t, :], in_=board[t][:].indirect(l5[:]), func=COPY, scale=sa_sb[:, t : t + 1])

        xr_sc = tile([P, O], U8, "xr_sc", "a2")
        nc.vector.tensor_copy(xr_sc[:], xr_plane[:].indirect(l7[:]))
        xr_codes = tile([P, O], U32, "xr_codes", "a3")
        nc.vector.tensor_copy(xr_codes[:], xr_sb[:].bitcast(U32).indirect(l7[:]))
        accs = [psum.tile([P, O], F32, name="ps_y%d" % u) for u in range(2)]
        for u in range(2):
            nc.tensor.matmul_mx(
                out=accs[u][:], lhsT=ws_sb[:, u * P : (u + 1) * P].bitcast(FP8X4),
                lhsT_scale=out_planes[:, N + u * P : N + (u + 1) * P],
                rhs=xr_codes[:].bitcast(FP8X4), rhs_scale=xr_sc[:], start=True, stop=False,
            )

        hid_bf = tile([P, O * PACK], BF16, "hid_bf")
        nc.vector.tensor_tensor(
            hid_bf[:].rearrange("p (c i t) -> p c t i", i=4, t=PACK),
            first[:].rearrange("p t (c i) -> p c t i", i=4),
            second[:].rearrange("p t (c i) -> p c t i", i=4),
            MAX,
        )
        hid_codes = tile([P, O], U32, "hid_codes")
        hid_sc = tile([P, O], U8, "hid_sc")
        nc.vector.quantize_mx(out=hid_codes[:].bitcast(FP8X4), scales=hid_sc[:], in_=hid_bf[:])

        for u in range(2):
            nc.tensor.matmul_mx(
                out=accs[u][:], lhsT=wb_sb[:, 2 * P * u : 2 * P * (u + 1)].bitcast(FP4X4),
                lhsT_scale=out_planes[:, u * P : (u + 1) * P],
                rhs=hid_codes[:].bitcast(FP8X4), rhs_scale=hid_sc[:], start=False, stop=True,
            )
        y0 = tile([P, O], F32, "y0")
        nc.vector.tensor_copy(y0[:], accs[0][:])
        nc.sync.dma_start(out[0:P, :], y0[:])
        y1 = tile([P, O], F32, "y1")
        nc.scalar.copy(y1[:], accs[1][:])
        nc.scalar.dma_start(out[P : 2 * P, :], y1[:])
